import numpy as np
import ml_dtypes


def mxq(x, axis, fmt="e4m3"):
    dtype, down = {"e4m3": (ml_dtypes.float8_e4m3fn, 7), "e5m2": (ml_dtypes.float8_e5m2, 14)}[fmt]
    v = np.moveaxis(np.asarray(x, np.float32).astype(ml_dtypes.bfloat16).astype(np.float64), axis, -1)
    blocks = v.reshape(v.shape[:-1] + (-1, 32))
    amax = np.abs(blocks).max(-1, keepdims=True)
    byte = np.maximum(np.where(amax > 0, np.frexp(amax)[1] - 1 + 127, 0) - down, 1)
    scale = np.exp2(byte - 127.0)
    codes = (blocks / scale).astype(np.float32).astype(dtype).astype(np.float64)
    return np.moveaxis((codes * scale).reshape(v.shape), -1, axis)


WIDE = False


def mx_kscale(k):
    if not WIDE:
        return np.ones(k)
    levels = np.array([10, -10, 5, -5, 0])
    if k % 512:
        return np.exp2(np.random.permutation(np.resize(levels, k // 32))).repeat(32)
    a = np.empty((k // 512, 16))
    for p in range(k // 512):
        a[p, :8] = np.random.permutation(np.resize(levels, 8))
        for g in range(8):
            far = levels[np.abs(levels - a[p, g]) >= 10]
            a[p, g + 8] = far[np.random.randint(len(far))]
    return np.exp2(a.ravel()).repeat(32)


def f64(x):
    return np.asarray(x).astype(np.float64)


def striped8(idx):
    return np.asarray(idx).reshape(8, -1, 16).transpose(0, 2, 1).reshape(128, -1).astype(np.uint16)


def unstriped8(offs):
    return offs.reshape(8, 16, -1).transpose(0, 2, 1).reshape(8, -1).astype(np.int64)


def pick8(x, idx, run):
    r = np.arange(len(x))
    return x[r[:, None], idx[r % (8 * run) // run]]


E2M1 = np.array([0.0, 0.5, 1.0, 1.5, 2.0, 3.0, 4.0, 6.0, -0.0, -0.5, -1.0, -1.5, -2.0, -3.0, -4.0, -6.0])


def pack_weight(w, fmt):
    k, n = w.shape
    w = f64(np.asarray(w, np.float32).astype(ml_dtypes.bfloat16)).reshape(k // 32, 32, n)
    amax = np.abs(w).max(1)
    if fmt == "e4m3":
        byte = np.frexp(amax)[1] - 1 + 127 - 7
    else:
        mant, ex = np.frexp(amax / 6.0)
        byte = np.where(mant > 0.5, ex, ex - 1) + 127
    byte = np.clip(np.where(amax > 0, byte, 1), 1, 254)
    scaled = (w * np.exp2(127.0 - byte)[:, None, :]).reshape(k, n).astype(np.float32)
    by_word = np.ascontiguousarray(scaled.reshape(k // 512, 128, 4, n).transpose(0, 1, 3, 2))
    if fmt == "e4m3":
        words = by_word.astype(ml_dtypes.float8_e4m3fn).view(np.uint8)
    else:
        c = by_word.astype(ml_dtypes.float4_e2m1fn).view(np.uint8) & 0xF
        words = (c[..., 0::2] | (c[..., 1::2] << 4)).reshape(k // 512, 128, 2 * n)
    return np.ascontiguousarray(words), np.ascontiguousarray(byte.astype(np.uint8).reshape(k // 512, 16, n))


def unpack_weight(words, scales, fmt):
    g, _, n = scales.shape
    words = np.ascontiguousarray(words).reshape(g, 128, n, -1)
    if fmt == "e4m3":
        vals = words.view(ml_dtypes.float8_e4m3fn).astype(np.float64)
    else:
        nib = np.empty((g, 128, n, 4), np.uint8)
        nib[..., 0::2] = words & 0xF
        nib[..., 1::2] = words >> 4
        vals = E2M1[nib]
    vals = vals * np.repeat(np.exp2(scales.astype(np.float64) - 127.0), 8, axis=1)[..., None]
    return vals.transpose(0, 1, 3, 2).reshape(g * 512, n)


D, K, T, Z, I, Q = 512, 512, 1024, 1024, 512, 128


def setup_inputs():
    n = np.random.standard_normal
    idx = np.stack([np.random.permutation(T)[:I] for _ in range(8)])
    idx2 = np.stack([np.random.permutation(Z)[:I] for _ in range(8)])
    idx3 = np.stack([np.random.permutation(Z)[:I] for _ in range(8)])
    fd = mx_kscale(D)
    fk = mx_kscale(K)
    wqp = pack_weight(n((D, K)) * 1.0 / np.sqrt(D) * fd[:, None] * fk, "e4m3")
    keysp = pack_weight(n((K, T)) * 1.0 / np.sqrt(K) / fk[:, None], "e2m1")
    tagsp = pack_weight(n((D, T)) * 0.5 / np.sqrt(D) * fd[:, None], "e4m3")
    return {
        "states": (n((D, Q)) * 0.95 / fd[:, None]).astype(np.float32),
        "wq_words": wqp[0],
        "wq_scales": wqp[1],
        "keys_words": keysp[0],
        "keys_scales": keysp[1],
        "tags_words": tagsp[0],
        "tags_scales": tagsp[1],
        "old": (1.0 * n((Q, Z))).astype(np.float32),
        "lam": (np.random.uniform(0.5, 1.5, (Q, 1))).astype(np.float32),
        "offs": striped8(idx),
        "offs2": striped8(idx2),
        "offs3": striped8(idx3),
    }


def reference(states, wq_words, wq_scales, keys_words, keys_scales, tags_words, tags_scales, old, lam, offs, offs2, offs3):
    idx = unstriped8(offs)
    idx2 = unstriped8(offs2)
    idx3 = unstriped8(offs3)
    wqu = unpack_weight(wq_words, wq_scales, "e4m3")
    keysu = unpack_weight(keys_words, keys_scales, "e2m1")
    tagsu = unpack_weight(tags_words, tags_scales, "e4m3")
    statesq = mxq(f64(states), 0, "e4m3")
    qv = wqu.T @ statesq
    qvq = mxq(qv, 0, "e4m3")
    a = qvq.T @ keysu + statesq.T @ tagsu
    w = pick8(a, idx, 16) - pick8(f64(old), idx2, 16)
    f1 = np.zeros((Q, Z))
    f1[np.arange(Q)[:, None], idx2[np.arange(Q) % 128 // 16]] = w
    cc = f64(old) + f1 * f64(lam)
    y = pick8(cc, idx3, 16)
    return y

@@ -1,0 +1,158 @@
+from contextlib import ExitStack
+
+import concourse.mybir as mybir
+
+D, K, T, Z, I, Q = 512, 512, 1024, 1024, 512, 128
+FLOPS = 2 * (D * K * Q + K * Q * T + D * Q * T)
+
+F32 = mybir.dt.float32
+BF16 = mybir.dt.bfloat16
+I32 = mybir.dt.int32
+U32 = mybir.dt.uint32
+U16 = mybir.dt.uint16
+U8 = mybir.dt.uint8
+FP8X4 = mybir.dt.float8_e4m3fn_x4
+FP4X4 = mybir.dt.float4_e2m1fn_x4
+ALU = mybir.AluOpType
+COPY = mybir.ActivationFunctionType.Copy
+
+P = 128
+PACK = 4
+BANKS = 4
+NB = T // BANKS
+HALF = I // 2
+LIST_HALF = HALF // 16
+QV = 96
+
+
+def load_scale_quadrant(queue, plane, scales, quadrant):
+    queue.dma_start(
+        out=plane[32 * quadrant : 32 * quadrant + 4, :].bitcast(I32),
+        in_=scales[0, 4 * quadrant : 4 * quadrant + 4, :].bitcast(I32),
+    )
+
+
+def tile_attend_rebased_madeparts_kernel(
+    tc, states, wq_words, wq_scales, keys_words, keys_scales, tags_words, tags_scales,
+    old, lam, offs, offs2, offs3, out,
+):
+    nc = tc.nc
+    with ExitStack() as ctx:
+        sb = ctx.enter_context(tc.tile_pool(name="sb", bufs=1))
+        ps = ctx.enter_context(tc.psum_pool(name="ps", bufs=1))
+
+        states_raw = sb.tile([P, PACK, Q], F32)
+        wq_raw = sb.tile([P, K], U32, align_bytes=64)
+        wq_plane_raw = sb.tile([P, K], U8, align_bytes=64)
+        keys = sb.tile([P, 2 * T], U8, align_bytes=64)
+        keys_plane = sb.tile([P, T], U8, align_bytes=64)
+        tags = sb.tile([P, T], U32, align_bytes=64)
+        tags_plane = sb.tile([P, T], U8, align_bytes=64)
+        old_sb = sb.tile([P, Z], F32)
+        lam_sb = sb.tile([P, 1], F32)
+        list_a = sb.tile([P, I // 16], U16)
+        list_old = sb.tile([P, I // 16], U16)
+        list_cc = sb.tile([P, I // 16], U16)
+        f1 = sb.tile([P, Z], F32)
+
+        nc.vector.memset(wq_plane_raw[:].bitcast(I32), 0)
+        nc.vector.memset(keys_plane[:].bitcast(I32), 0)
+        nc.vector.memset(tags_plane[:].bitcast(I32), 0)
+        nc.vector.memset(f1[:], 0.0)
+
+        nc.sync.dma_start(out=states_raw[:], in_=states.rearrange("(p j) q -> p j q", j=PACK))
+        nc.sync.dma_start(
+            out=wq_raw[:].bitcast(I32),
+            in_=wq_words[0].rearrange("p n t -> p (n t)").bitcast(I32),
+        )
+        for quadrant in range(4):
+            load_scale_quadrant(nc.sync, wq_plane_raw, wq_scales, quadrant)
+        nc.sync.dma_start(out=old_sb[:], in_=old)
+        nc.sync.dma_start(out=list_old[:], in_=offs2)
+        nc.sync.dma_start(
+            out=tags[:].bitcast(I32),
+            in_=tags_words[0].rearrange("p n t -> p (n t)").bitcast(I32),
+        )
+        for quadrant in range(4):
+            load_scale_quadrant(nc.sync, tags_plane, tags_scales, quadrant)
+        nc.sync.dma_start(out=keys[:].bitcast(I32), in_=keys_words[0].bitcast(I32))
+        for quadrant in range(2):
+            load_scale_quadrant(nc.sync, keys_plane, keys_scales, quadrant)
+        nc.sync.dma_start(out=list_a[:], in_=offs)
+        nc.sync.dma_start(out=list_cc[:], in_=offs3)
+        for quadrant in range(2, 4):
+            load_scale_quadrant(nc.gpsimd, keys_plane, keys_scales, quadrant)
+        nc.gpsimd.dma_start(out=lam_sb[:], in_=lam)
+
+        states_bf = sb.tile([P, Q, PACK], BF16, align_bytes=64)
+        nc.vector.tensor_copy(out=states_bf[:, :QV, :], in_=states_raw[:, :, :QV].rearrange("p j q -> p q j"))
+        nc.scalar.activation(out=states_bf[:, QV:, :], in_=states_raw[:, :, QV:].rearrange("p j q -> p q j"), func=COPY)
+        wq_dealt = sb.tile([P, PACK, P], U32, align_bytes=64)
+        for pair in range(2):
+            places = slice(2 * pair, 2 * pair + 2)
+            nc.scalar.copy(out=wq_dealt[:, places, :], in_=wq_raw[:].rearrange("p (m t) -> p t m", t=PACK)[:, places, :])
+        wq_plane = sb.tile([P, PACK, P], U8, align_bytes=64)
+        for pair in range(2):
+            places = slice(2 * pair, 2 * pair + 2)
+            nc.vector.tensor_copy(
+                out=wq_plane[:, places, :], in_=wq_plane_raw[:].rearrange("p (m t) -> p t m", t=PACK)[:, places, :]
+            )
+        states_q = sb.tile([P, Q], U32, align_bytes=64)
+        states_plane = sb.tile([P, Q], U8, align_bytes=64)
+        nc.vector.quantize_mx(
+            out=states_q[:].bitcast(FP8X4), scales=states_plane[:],
+            in_=states_bf[:].rearrange("p q j -> p (q j)"),
+        )
+
+        qv_ps = ps.tile([P, PACK, Q], F32)
+        for t in range(PACK):
+            nc.tensor.matmul_mx(
+                out=qv_ps[:, t, :], lhsT=wq_dealt[:, t, :].bitcast(FP8X4), lhsT_scale=wq_plane[:, t, :],
+                rhs=states_q[:].bitcast(FP8X4), rhs_scale=states_plane[:], start=True, stop=True,
+            )
+        a_ps = [ps.tile([P, NB], F32, name="a_ps%d" % b) for b in range(BANKS)]
+        for b in range(BANKS):
+            cols = slice(b * NB, (b + 1) * NB)
+            nc.tensor.matmul_mx(
+                out=a_ps[b][:], lhsT=states_q[:].bitcast(FP8X4), lhsT_scale=states_plane[:],
+                rhs=tags[:, cols].bitcast(FP8X4), rhs_scale=tags_plane[:, cols], start=True, stop=False,
+            )
+
+        qv_bf = sb.tile([P, Q, PACK], BF16, align_bytes=64)
+        nc.vector.tensor_copy(out=qv_bf[:], in_=qv_ps[:].rearrange("p t q -> p q t"))
+        qv_q = sb.tile([P, Q], U32, align_bytes=64)
+        qv_plane = sb.tile([P, Q], U8, align_bytes=64)
+        nc.vector.quantize_mx(
+            out=qv_q[:].bitcast(FP8X4), scales=qv_plane[:], in_=qv_bf[:].rearrange("p q t -> p (q t)"),
+        )
+
+        neg_old = sb.tile([P, I], F32)
+        nc.scalar.activation(out=neg_old[:], in_=old_sb[:].indirect(list_old[:]), func=COPY, scale=-1.0)
+
+        a_sb = sb.tile([P, T], F32)
+        for b in range(BANKS):
+            cols = slice(b * NB, (b + 1) * NB)
+            nc.tensor.matmul_mx(
+                out=a_ps[b][:], lhsT=qv_q[:].bitcast(FP8X4), lhsT_scale=qv_plane[:],
+                rhs=keys[:, 2 * b * NB : 2 * (b + 1) * NB].bitcast(FP4X4), rhs_scale=keys_plane[:, cols],
+                start=False, stop=True,
+            )
+            if b % 2 == 0:
+                nc.vector.tensor_copy(out=a_sb[:, cols], in_=a_ps[b][:])
+            else:
+                nc.scalar.copy(out=a_sb[:, cols], in_=a_ps[b][:])
+
+        a_listed = sb.tile([P, I], F32)
+        nc.vector.tensor_copy(out=a_listed[:, :HALF], in_=a_sb[:].indirect(list_a[:, :LIST_HALF]))
+        nc.scalar.activation(out=a_listed[:, HALF:], in_=a_sb[:].indirect(list_a[:, LIST_HALF:]), func=COPY)
+        nc.vector.tensor_tensor(out=f1[:].indirect(list_old[:]), in0=a_listed[:], in1=neg_old[:], op=ALU.add)
+
+        cc = sb.tile([P, Z], F32)
+        nc.vector.scalar_tensor_tensor(
+            out=cc[:], in0=f1[:], scalar=lam_sb[:], in1=old_sb[:], op0=ALU.mult, op1=ALU.add,
+        )
+        y = sb.tile([P, I], F32)
+        nc.vector.tensor_copy(out=y[:, :HALF], in_=cc[:].indirect(list_cc[:, :LIST_HALF]))
+        nc.sync.dma_start(out=out[:, :HALF], in_=y[:, :HALF])
+        nc.scalar.activation(out=y[:, HALF:], in_=cc[:].indirect(list_cc[:, LIST_HALF:]), func=COPY)
+        nc.scalar.dma_start(out=out[:, HALF:], in_=y[:, HALF:])

@@ -23,6 +23,7 @@ NB = T // BANKS
 HALF = I // 2
 LIST_HALF = HALF // 16
 QV = 96
+MS = 80
 
 
 def load_scale_quadrant(queue, plane, scales, quadrant):
@@ -43,7 +44,7 @@ def tile_attend_rebased_madeparts_kernel(
 
         states_raw = sb.tile([P, PACK, Q], F32)
         wq_raw = sb.tile([P, K], U32, align_bytes=64)
-        wq_plane_raw = sb.tile([P, K], U8, align_bytes=64)
+        wq_plane_raw = sb.tile([P, K], U8, align_bytes=64, tag="shared")
         keys = sb.tile([P, 2 * T], U8, align_bytes=64)
         keys_plane = sb.tile([P, T], U8, align_bytes=64)
         tags = sb.tile([P, T], U32, align_bytes=64)
@@ -53,44 +54,45 @@ def tile_attend_rebased_madeparts_kernel(
         list_a = sb.tile([P, I // 16], U16)
         list_old = sb.tile([P, I // 16], U16)
         list_cc = sb.tile([P, I // 16], U16)
-        f1 = sb.tile([P, Z], F32)
 
         nc.vector.memset(wq_plane_raw[:].bitcast(I32), 0)
-        nc.vector.memset(keys_plane[:].bitcast(I32), 0)
         nc.vector.memset(tags_plane[:].bitcast(I32), 0)
-        nc.vector.memset(f1[:], 0.0)
+        nc.vector.memset(keys_plane[:].bitcast(I32), 0)
 
         nc.sync.dma_start(out=states_raw[:], in_=states.rearrange("(p j) q -> p j q", j=PACK))
+        for quadrant in range(2):
+            load_scale_quadrant(nc.sync, wq_plane_raw, wq_scales, quadrant)
         nc.sync.dma_start(
             out=wq_raw[:].bitcast(I32),
             in_=wq_words[0].rearrange("p n t -> p (n t)").bitcast(I32),
         )
-        for quadrant in range(4):
+        for quadrant in range(2, 4):
             load_scale_quadrant(nc.sync, wq_plane_raw, wq_scales, quadrant)
-        nc.sync.dma_start(out=old_sb[:], in_=old)
-        nc.sync.dma_start(out=list_old[:], in_=offs2)
         nc.sync.dma_start(
             out=tags[:].bitcast(I32),
             in_=tags_words[0].rearrange("p n t -> p (n t)").bitcast(I32),
         )
-        for quadrant in range(4):
+        for quadrant in range(3):
             load_scale_quadrant(nc.sync, tags_plane, tags_scales, quadrant)
+        nc.sync.dma_start(out=old_sb[:], in_=old)
+        nc.sync.dma_start(out=list_old[:], in_=offs2)
         nc.sync.dma_start(out=keys[:].bitcast(I32), in_=keys_words[0].bitcast(I32))
-        for quadrant in range(2):
+        for quadrant in range(4):
             load_scale_quadrant(nc.sync, keys_plane, keys_scales, quadrant)
         nc.sync.dma_start(out=list_a[:], in_=offs)
         nc.sync.dma_start(out=list_cc[:], in_=offs3)
-        for quadrant in range(2, 4):
-            load_scale_quadrant(nc.gpsimd, keys_plane, keys_scales, quadrant)
-        nc.gpsimd.dma_start(out=lam_sb[:], in_=lam)
+        nc.sync.dma_start(out=lam_sb[:], in_=lam)
+        load_scale_quadrant(nc.gpsimd, tags_plane, tags_scales, 3)
 
         states_bf = sb.tile([P, Q, PACK], BF16, align_bytes=64)
         nc.vector.tensor_copy(out=states_bf[:, :QV, :], in_=states_raw[:, :, :QV].rearrange("p j q -> p q j"))
         nc.scalar.activation(out=states_bf[:, QV:, :], in_=states_raw[:, :, QV:].rearrange("p j q -> p q j"), func=COPY)
         wq_dealt = sb.tile([P, PACK, P], U32, align_bytes=64)
-        for pair in range(2):
-            places = slice(2 * pair, 2 * pair + 2)
-            nc.scalar.copy(out=wq_dealt[:, places, :], in_=wq_raw[:].rearrange("p (m t) -> p t m", t=PACK)[:, places, :])
+        wq_by_row = wq_raw[:].rearrange("p (m t) -> p m t", t=PACK)
+        nc.scalar.copy(out=wq_dealt[:, :, :MS].rearrange("p t m -> p m t"), in_=wq_by_row[:, :MS, :])
+        nc.vector.tensor_copy(
+            out=wq_dealt[:].bitcast(I32)[:, :, MS:].rearrange("p t m -> p m t"), in_=wq_by_row.bitcast(I32)[:, MS:, :]
+        )
         wq_plane = sb.tile([P, PACK, P], U8, align_bytes=64)
         for pair in range(2):
             places = slice(2 * pair, 2 * pair + 2)
@@ -103,6 +105,9 @@ def tile_attend_rebased_madeparts_kernel(
             out=states_q[:].bitcast(FP8X4), scales=states_plane[:],
             in_=states_bf[:].rearrange("p q j -> p (q j)"),
         )
+
+        f1 = sb.tile([P, Z], F32, align_bytes=64, tag="shared")
+        nc.vector.memset(f1[:], 0.0)
 
         qv_ps = ps.tile([P, PACK, Q], F32)
         for t in range(PACK):
@@ -127,7 +132,11 @@ def tile_attend_rebased_madeparts_kernel(
         )
 
         neg_old = sb.tile([P, I], F32)
-        nc.scalar.activation(out=neg_old[:], in_=old_sb[:].indirect(list_old[:]), func=COPY, scale=-1.0)
+        nc.scalar.activation(out=neg_old[:, :HALF], in_=old_sb[:].indirect(list_old[:, :LIST_HALF]), func=COPY, scale=-1.0)
+        nc.vector.tensor_scalar(
+            out=neg_old[:, HALF:], in0=old_sb[:].indirect(list_old[:, LIST_HALF:]),
+            scalar1=-1.0, scalar2=0.0, op0=ALU.mult, op1=ALU.add,
+        )
 
         a_sb = sb.tile([P, T], F32)
         for b in range(BANKS):

@@ -18,8 +18,8 @@ COPY = mybir.ActivationFunctionType.Copy
 
 P = 128
 PACK = 4
-BANKS = 4
-NB = T // BANKS
+WIDTHS = (256, 256, 256, 256)
+PIECES = [slice(sum(WIDTHS[:b]), sum(WIDTHS[: b + 1])) for b in range(len(WIDTHS))]
 HALF = I // 2
 LIST_HALF = HALF // 16
 QV = 96
@@ -44,8 +44,8 @@ def tile_attend_rebased_madeparts_kernel(
 
         states_raw = sb.tile([P, PACK, Q], F32)
         wq_raw = sb.tile([P, K], U32, align_bytes=64)
-        wq_plane_raw = sb.tile([P, K], U8, align_bytes=64, tag="shared")
-        keys = sb.tile([P, 2 * T], U8, align_bytes=64)
+        wq_plane_raw = sb.tile([P, K], U8, align_bytes=64)
+        keys = sb.tile([P, 2 * T], U8, align_bytes=64, tag="keys")
         keys_plane = sb.tile([P, T], U8, align_bytes=64)
         tags = sb.tile([P, T], U32, align_bytes=64)
         tags_plane = sb.tile([P, T], U8, align_bytes=64)
@@ -58,6 +58,8 @@ def tile_attend_rebased_madeparts_kernel(
         nc.vector.memset(wq_plane_raw[:].bitcast(I32), 0)
         nc.vector.memset(tags_plane[:].bitcast(I32), 0)
         nc.vector.memset(keys_plane[:].bitcast(I32), 0)
+        f1 = sb.tile([P, Z], F32)
+        nc.vector.memset(f1[:], 0.0)
 
         nc.sync.dma_start(out=states_raw[:], in_=states.rearrange("(p j) q -> p j q", j=PACK))
         for quadrant in range(2):
@@ -68,21 +70,23 @@ def tile_attend_rebased_madeparts_kernel(
         )
         for quadrant in range(2, 4):
             load_scale_quadrant(nc.sync, wq_plane_raw, wq_scales, quadrant)
+        load_scale_quadrant(nc.sync, tags_plane, tags_scales, 0)
         nc.sync.dma_start(
             out=tags[:].bitcast(I32),
             in_=tags_words[0].rearrange("p n t -> p (n t)").bitcast(I32),
         )
-        for quadrant in range(3):
+        for quadrant in range(1, 3):
             load_scale_quadrant(nc.sync, tags_plane, tags_scales, quadrant)
+        nc.sync.dma_start(out=keys[:].bitcast(I32), in_=keys_words[0].bitcast(I32))
+        for quadrant in range(3):
+            load_scale_quadrant(nc.sync, keys_plane, keys_scales, quadrant)
         nc.sync.dma_start(out=old_sb[:], in_=old)
         nc.sync.dma_start(out=list_old[:], in_=offs2)
-        nc.sync.dma_start(out=keys[:].bitcast(I32), in_=keys_words[0].bitcast(I32))
-        for quadrant in range(4):
-            load_scale_quadrant(nc.sync, keys_plane, keys_scales, quadrant)
         nc.sync.dma_start(out=list_a[:], in_=offs)
         nc.sync.dma_start(out=list_cc[:], in_=offs3)
         nc.sync.dma_start(out=lam_sb[:], in_=lam)
         load_scale_quadrant(nc.gpsimd, tags_plane, tags_scales, 3)
+        load_scale_quadrant(nc.gpsimd, keys_plane, keys_scales, 3)
 
         states_bf = sb.tile([P, Q, PACK], BF16, align_bytes=64)
         nc.vector.tensor_copy(out=states_bf[:, :QV, :], in_=states_raw[:, :, :QV].rearrange("p j q -> p q j"))
@@ -106,55 +110,52 @@ def tile_attend_rebased_madeparts_kernel(
             in_=states_bf[:].rearrange("p q j -> p (q j)"),
         )
 
-        f1 = sb.tile([P, Z], F32, align_bytes=64, tag="shared")
-        nc.vector.memset(f1[:], 0.0)
-
-        qv_ps = ps.tile([P, PACK, Q], F32)
+        qv_ps = [ps.tile([P, 2, Q], F32, name="qv_ps%d" % pair) for pair in range(2)]
         for t in range(PACK):
             nc.tensor.matmul_mx(
-                out=qv_ps[:, t, :], lhsT=wq_dealt[:, t, :].bitcast(FP8X4), lhsT_scale=wq_plane[:, t, :],
+                out=qv_ps[t // 2][:, t % 2, :], lhsT=wq_dealt[:, t, :].bitcast(FP8X4), lhsT_scale=wq_plane[:, t, :],
                 rhs=states_q[:].bitcast(FP8X4), rhs_scale=states_plane[:], start=True, stop=True,
             )
-        a_ps = [ps.tile([P, NB], F32, name="a_ps%d" % b) for b in range(BANKS)]
-        for b in range(BANKS):
-            cols = slice(b * NB, (b + 1) * NB)
+        a_ps = [ps.tile([P, width], F32, name="a_ps%d" % b) for b, width in enumerate(WIDTHS)]
+        for b, cols in enumerate(PIECES):
             nc.tensor.matmul_mx(
                 out=a_ps[b][:], lhsT=states_q[:].bitcast(FP8X4), lhsT_scale=states_plane[:],
                 rhs=tags[:, cols].bitcast(FP8X4), rhs_scale=tags_plane[:, cols], start=True, stop=False,
             )
 
         qv_bf = sb.tile([P, Q, PACK], BF16, align_bytes=64)
-        nc.vector.tensor_copy(out=qv_bf[:], in_=qv_ps[:].rearrange("p t q -> p q t"))
+        nc.scalar.copy(out=qv_bf[:, :, :2], in_=qv_ps[0][:].rearrange("p t q -> p q t"))
+        nc.vector.tensor_copy(out=qv_bf[:, :, 2:], in_=qv_ps[1][:].rearrange("p t q -> p q t"))
         qv_q = sb.tile([P, Q], U32, align_bytes=64)
         qv_plane = sb.tile([P, Q], U8, align_bytes=64)
         nc.vector.quantize_mx(
             out=qv_q[:].bitcast(FP8X4), scales=qv_plane[:], in_=qv_bf[:].rearrange("p q t -> p (q t)"),
         )
 
-        neg_old = sb.tile([P, I], F32)
-        nc.scalar.activation(out=neg_old[:, :HALF], in_=old_sb[:].indirect(list_old[:, :LIST_HALF]), func=COPY, scale=-1.0)
-        nc.vector.tensor_scalar(
-            out=neg_old[:, HALF:], in0=old_sb[:].indirect(list_old[:, LIST_HALF:]),
-            scalar1=-1.0, scalar2=0.0, op0=ALU.mult, op1=ALU.add,
-        )
-
         a_sb = sb.tile([P, T], F32)
-        for b in range(BANKS):
-            cols = slice(b * NB, (b + 1) * NB)
+        for b, cols in enumerate(PIECES):
             nc.tensor.matmul_mx(
                 out=a_ps[b][:], lhsT=qv_q[:].bitcast(FP8X4), lhsT_scale=qv_plane[:],
-                rhs=keys[:, 2 * b * NB : 2 * (b + 1) * NB].bitcast(FP4X4), rhs_scale=keys_plane[:, cols],
+                rhs=keys[:, 2 * cols.start : 2 * cols.stop].bitcast(FP4X4), rhs_scale=keys_plane[:, cols],
                 start=False, stop=True,
             )
-            if b % 2 == 0:
+            if b in (0, 2):
                 nc.vector.tensor_copy(out=a_sb[:, cols], in_=a_ps[b][:])
             else:
                 nc.scalar.copy(out=a_sb[:, cols], in_=a_ps[b][:])
 
         a_listed = sb.tile([P, I], F32)
+        neg_old = sb.tile([P, I], F32, align_bytes=64, tag="keys")
         nc.vector.tensor_copy(out=a_listed[:, :HALF], in_=a_sb[:].indirect(list_a[:, :LIST_HALF]))
+        nc.scalar.activation(out=neg_old[:, :HALF], in_=old_sb[:].indirect(list_old[:, :LIST_HALF]), func=COPY, scale=-1.0)
         nc.scalar.activation(out=a_listed[:, HALF:], in_=a_sb[:].indirect(list_a[:, LIST_HALF:]), func=COPY)
-        nc.vector.tensor_tensor(out=f1[:].indirect(list_old[:]), in0=a_listed[:], in1=neg_old[:], op=ALU.add)
+        nc.scalar.activation(out=neg_old[:, HALF:], in_=old_sb[:].indirect(list_old[:, LIST_HALF:]), func=COPY, scale=-1.0)
+        for h in range(2):
+            slots = slice(h * HALF, (h + 1) * HALF)
+            nc.vector.tensor_tensor(
+                out=f1[:].indirect(list_old[:, h * LIST_HALF : (h + 1) * LIST_HALF]),
+                in0=a_listed[:, slots], in1=neg_old[:, slots], op=ALU.add,
+            )
 
         cc = sb.tile([P, Z], F32)
         nc.vector.scalar_tensor_tensor(

from contextlib import ExitStack

import concourse.mybir as mybir

D, K, T, Z, I, Q = 512, 512, 1024, 1024, 512, 128
FLOPS = 2 * (D * K * Q + K * Q * T + D * Q * T)

F32 = mybir.dt.float32
BF16 = mybir.dt.bfloat16
I32 = mybir.dt.int32
U32 = mybir.dt.uint32
U16 = mybir.dt.uint16
U8 = mybir.dt.uint8
FP8X4 = mybir.dt.float8_e4m3fn_x4
FP4X4 = mybir.dt.float4_e2m1fn_x4
ALU = mybir.AluOpType
COPY = mybir.ActivationFunctionType.Copy

P = 128
PACK = 4
WIDTHS = (256, 256, 256, 256)
PIECES = [slice(sum(WIDTHS[:b]), sum(WIDTHS[: b + 1])) for b in range(len(WIDTHS))]
HALF = I // 2
LIST_HALF = HALF // 16
QV = 96
MS = 80


def load_scale_quadrant(queue, plane, scales, quadrant):
    queue.dma_start(
        out=plane[32 * quadrant : 32 * quadrant + 4, :].bitcast(I32),
        in_=scales[0, 4 * quadrant : 4 * quadrant + 4, :].bitcast(I32),
    )


def tile_attend_rebased_madeparts_kernel(
    tc, states, wq_words, wq_scales, keys_words, keys_scales, tags_words, tags_scales,
    old, lam, offs, offs2, offs3, out,
):
    nc = tc.nc
    with ExitStack() as ctx:
        sb = ctx.enter_context(tc.tile_pool(name="sb", bufs=1))
        ps = ctx.enter_context(tc.psum_pool(name="ps", bufs=1))

        states_raw = sb.tile([P, PACK, Q], F32)
        wq_raw = sb.tile([P, K], U32, align_bytes=64)
        wq_plane_raw = sb.tile([P, K], U8, align_bytes=64)
        keys = sb.tile([P, 2 * T], U8, align_bytes=64, tag="keys")
        keys_plane = sb.tile([P, T], U8, align_bytes=64)
        tags = sb.tile([P, T], U32, align_bytes=64)
        tags_plane = sb.tile([P, T], U8, align_bytes=64)
        old_sb = sb.tile([P, Z], F32)
        lam_sb = sb.tile([P, 1], F32)
        list_a = sb.tile([P, I // 16], U16)
        list_old = sb.tile([P, I // 16], U16)
        list_cc = sb.tile([P, I // 16], U16)

        nc.vector.memset(wq_plane_raw[:].bitcast(I32), 0)
        nc.vector.memset(tags_plane[:].bitcast(I32), 0)
        nc.vector.memset(keys_plane[:].bitcast(I32), 0)
        f1 = sb.tile([P, Z], F32)
        nc.vector.memset(f1[:], 0.0)

        nc.sync.dma_start(out=states_raw[:], in_=states.rearrange("(p j) q -> p j q", j=PACK))
        for quadrant in range(2):
            load_scale_quadrant(nc.sync, wq_plane_raw, wq_scales, quadrant)
        nc.sync.dma_start(
            out=wq_raw[:].bitcast(I32),
            in_=wq_words[0].rearrange("p n t -> p (n t)").bitcast(I32),
        )
        for quadrant in range(2, 4):
            load_scale_quadrant(nc.sync, wq_plane_raw, wq_scales, quadrant)
        load_scale_quadrant(nc.sync, tags_plane, tags_scales, 0)
        nc.sync.dma_start(
            out=tags[:].bitcast(I32),
            in_=tags_words[0].rearrange("p n t -> p (n t)").bitcast(I32),
        )
        for quadrant in range(1, 3):
            load_scale_quadrant(nc.sync, tags_plane, tags_scales, quadrant)
        nc.sync.dma_start(out=keys[:].bitcast(I32), in_=keys_words[0].bitcast(I32))
        for quadrant in range(3):
            load_scale_quadrant(nc.sync, keys_plane, keys_scales, quadrant)
        nc.sync.dma_start(out=old_sb[:], in_=old)
        nc.sync.dma_start(out=list_old[:], in_=offs2)
        nc.sync.dma_start(out=list_a[:], in_=offs)
        nc.sync.dma_start(out=list_cc[:], in_=offs3)
        nc.sync.dma_start(out=lam_sb[:], in_=lam)
        load_scale_quadrant(nc.gpsimd, tags_plane, tags_scales, 3)
        load_scale_quadrant(nc.gpsimd, keys_plane, keys_scales, 3)

        states_bf = sb.tile([P, Q, PACK], BF16, align_bytes=64)
        nc.vector.tensor_copy(out=states_bf[:, :QV, :], in_=states_raw[:, :, :QV].rearrange("p j q -> p q j"))
        nc.scalar.activation(out=states_bf[:, QV:, :], in_=states_raw[:, :, QV:].rearrange("p j q -> p q j"), func=COPY)
        wq_dealt = sb.tile([P, PACK, P], U32, align_bytes=64)
        wq_by_row = wq_raw[:].rearrange("p (m t) -> p m t", t=PACK)
        nc.scalar.copy(out=wq_dealt[:, :, :MS].rearrange("p t m -> p m t"), in_=wq_by_row[:, :MS, :])
        nc.vector.tensor_copy(
            out=wq_dealt[:].bitcast(I32)[:, :, MS:].rearrange("p t m -> p m t"), in_=wq_by_row.bitcast(I32)[:, MS:, :]
        )
        wq_plane = sb.tile([P, PACK, P], U8, align_bytes=64)
        for pair in range(2):
            places = slice(2 * pair, 2 * pair + 2)
            nc.vector.tensor_copy(
                out=wq_plane[:, places, :], in_=wq_plane_raw[:].rearrange("p (m t) -> p t m", t=PACK)[:, places, :]
            )
        states_q = sb.tile([P, Q], U32, align_bytes=64)
        states_plane = sb.tile([P, Q], U8, align_bytes=64)
        nc.vector.quantize_mx(
            out=states_q[:].bitcast(FP8X4), scales=states_plane[:],
            in_=states_bf[:].rearrange("p q j -> p (q j)"),
        )

        qv_ps = [ps.tile([P, 2, Q], F32, name="qv_ps%d" % pair) for pair in range(2)]
        for t in range(PACK):
            nc.tensor.matmul_mx(
                out=qv_ps[t // 2][:, t % 2, :], lhsT=wq_dealt[:, t, :].bitcast(FP8X4), lhsT_scale=wq_plane[:, t, :],
                rhs=states_q[:].bitcast(FP8X4), rhs_scale=states_plane[:], start=True, stop=True,
            )
        a_ps = [ps.tile([P, width], F32, name="a_ps%d" % b) for b, width in enumerate(WIDTHS)]
        for b, cols in enumerate(PIECES):
            nc.tensor.matmul_mx(
                out=a_ps[b][:], lhsT=states_q[:].bitcast(FP8X4), lhsT_scale=states_plane[:],
                rhs=tags[:, cols].bitcast(FP8X4), rhs_scale=tags_plane[:, cols], start=True, stop=False,
            )

        qv_bf = sb.tile([P, Q, PACK], BF16, align_bytes=64)
        nc.scalar.copy(out=qv_bf[:, :, :2], in_=qv_ps[0][:].rearrange("p t q -> p q t"))
        nc.vector.tensor_copy(out=qv_bf[:, :, 2:], in_=qv_ps[1][:].rearrange("p t q -> p q t"))
        qv_q = sb.tile([P, Q], U32, align_bytes=64)
        qv_plane = sb.tile([P, Q], U8, align_bytes=64)
        nc.vector.quantize_mx(
            out=qv_q[:].bitcast(FP8X4), scales=qv_plane[:], in_=qv_bf[:].rearrange("p q t -> p (q t)"),
        )

        a_sb = sb.tile([P, T], F32)
        for b, cols in enumerate(PIECES):
            nc.tensor.matmul_mx(
                out=a_ps[b][:], lhsT=qv_q[:].bitcast(FP8X4), lhsT_scale=qv_plane[:],
                rhs=keys[:, 2 * cols.start : 2 * cols.stop].bitcast(FP4X4), rhs_scale=keys_plane[:, cols],
                start=False, stop=True,
            )
            if b in (0, 2):
                nc.vector.tensor_copy(out=a_sb[:, cols], in_=a_ps[b][:])
            else:
                nc.scalar.copy(out=a_sb[:, cols], in_=a_ps[b][:])

        a_listed = sb.tile([P, I], F32)
        neg_old = sb.tile([P, I], F32, align_bytes=64, tag="keys")
        nc.vector.tensor_copy(out=a_listed[:, :HALF], in_=a_sb[:].indirect(list_a[:, :LIST_HALF]))
        nc.scalar.activation(out=neg_old[:, :HALF], in_=old_sb[:].indirect(list_old[:, :LIST_HALF]), func=COPY, scale=-1.0)
        nc.scalar.activation(out=a_listed[:, HALF:], in_=a_sb[:].indirect(list_a[:, LIST_HALF:]), func=COPY)
        nc.scalar.activation(out=neg_old[:, HALF:], in_=old_sb[:].indirect(list_old[:, LIST_HALF:]), func=COPY, scale=-1.0)
        for h in range(2):
            slots = slice(h * HALF, (h + 1) * HALF)
            nc.vector.tensor_tensor(
                out=f1[:].indirect(list_old[:, h * LIST_HALF : (h + 1) * LIST_HALF]),
                in0=a_listed[:, slots], in1=neg_old[:, slots], op=ALU.add,
            )

        cc = sb.tile([P, Z], F32)
        nc.vector.scalar_tensor_tensor(
            out=cc[:], in0=f1[:], scalar=lam_sb[:], in1=old_sb[:], op0=ALU.mult, op1=ALU.add,
        )
        y = sb.tile([P, I], F32)
        nc.vector.tensor_copy(out=y[:, :HALF], in_=cc[:].indirect(list_cc[:, :LIST_HALF]))
        nc.sync.dma_start(out=out[:, :HALF], in_=y[:, :HALF])
        nc.scalar.activation(out=y[:, HALF:], in_=cc[:].indirect(list_cc[:, LIST_HALF:]), func=COPY)
        nc.scalar.dma_start(out=out[:, HALF:], in_=y[:, HALF:])
